import numpy as np
import ml_dtypes


def mxq(x, axis, fmt="e4m3"):
    dtype, down = {"e4m3": (ml_dtypes.float8_e4m3fn, 7), "e5m2": (ml_dtypes.float8_e5m2, 14)}[fmt]
    v = np.moveaxis(np.asarray(x, np.float32).astype(ml_dtypes.bfloat16).astype(np.float64), axis, -1)
    blocks = v.reshape(v.shape[:-1] + (-1, 32))
    amax = np.abs(blocks).max(-1, keepdims=True)
    byte = np.maximum(np.where(amax > 0, np.frexp(amax)[1] - 1 + 127, 0) - down, 1)
    scale = np.exp2(byte - 127.0)
    codes = (blocks / scale).astype(np.float32).astype(dtype).astype(np.float64)
    return np.moveaxis((codes * scale).reshape(v.shape), -1, axis)


WIDE = False


def mx_kscale(k):
    if not WIDE:
        return np.ones(k)
    levels = np.array([30, -30])
    if k % 512:
        return np.exp2(np.random.permutation(np.resize(levels, k // 32))).repeat(32)
    a = np.empty((k // 512, 16))
    for p in range(k // 512):
        a[p, :8] = np.random.permutation(np.resize(levels, 8))
        for g in range(8):
            far = levels[np.abs(levels - a[p, g]) >= 10]
            a[p, g + 8] = far[np.random.randint(len(far))]
    return np.exp2(a.ravel()).repeat(32)


def f64(x):
    return np.asarray(x).astype(np.float64)


def striped(idx):
    return np.tile(np.asarray(idx).reshape(-1, 16).T, (8, 1)).astype(np.uint16)


def unstriped(offs):
    return offs[:16].T.reshape(-1).astype(np.int64)


E2M1 = np.array([0.0, 0.5, 1.0, 1.5, 2.0, 3.0, 4.0, 6.0, -0.0, -0.5, -1.0, -1.5, -2.0, -3.0, -4.0, -6.0])


def pack_weight(w, fmt):
    k, n = w.shape
    w = f64(np.asarray(w, np.float32).astype(ml_dtypes.bfloat16)).reshape(k // 32, 32, n)
    amax = np.abs(w).max(1)
    if fmt in ("e4m3", "e5m2"):
        byte = np.frexp(amax)[1] - 1 + 127 - (7 if fmt == "e4m3" else 14)
    else:
        mant, ex = np.frexp(amax / 6.0)
        byte = np.where(mant > 0.5, ex, ex - 1) + 127
    byte = np.clip(np.where(amax > 0, byte, 1), 1, 254)
    scaled = (w * np.exp2(127.0 - byte)[:, None, :]).reshape(k, n).astype(np.float32)
    by_word = np.ascontiguousarray(scaled.reshape(k // 512, 128, 4, n).transpose(0, 1, 3, 2))
    if fmt in ("e4m3", "e5m2"):
        words = by_word.astype(ml_dtypes.float8_e4m3fn if fmt == "e4m3" else ml_dtypes.float8_e5m2).view(np.uint8)
    else:
        c = by_word.astype(ml_dtypes.float4_e2m1fn).view(np.uint8) & 0xF
        words = (c[..., 0::2] | (c[..., 1::2] << 4)).reshape(k // 512, 128, 2 * n)
    return np.ascontiguousarray(words), np.ascontiguousarray(byte.astype(np.uint8).reshape(k // 512, 16, n))


def unpack_weight(words, scales, fmt):
    g, _, n = scales.shape
    words = np.ascontiguousarray(words).reshape(g, 128, n, -1)
    if fmt in ("e4m3", "e5m2"):
        vals = words.view(ml_dtypes.float8_e4m3fn if fmt == "e4m3" else ml_dtypes.float8_e5m2).astype(np.float64)
    else:
        nib = np.empty((g, 128, n, 4), np.uint8)
        nib[..., 0::2] = words & 0xF
        nib[..., 1::2] = words >> 4
        vals = E2M1[nib]
    vals = vals * np.repeat(np.exp2(scales.astype(np.float64) - 127.0), 8, axis=1)[..., None]
    return vals.transpose(0, 1, 3, 2).reshape(g * 512, n)


K, T, J, R, C, N = 512, 2048, 256, 512, 512, 256


def setup_inputs():
    n = np.random.standard_normal
    idx = np.random.permutation(T)[:J]
    idx2 = np.random.permutation(T)[:J]
    idx3 = np.random.permutation(C)[:J]
    idx4 = np.random.permutation(C)[:J]
    fk = mx_kscale(K)
    fr = mx_kscale(R)
    xtp = pack_weight(n((K, T)) / fk[:, None], "e2m1")
    wp = pack_weight(n((K, R)) * 1 / np.sqrt(K) * fk[:, None] * fr, "e5m2")
    w2p = pack_weight(n((K, R)) * 1 / np.sqrt(K) * fk[:, None] * fr, "e4m3")
    wbp = pack_weight(n((R, N)) * 1 / np.sqrt(R) / fr[:, None], "e4m3")
    wsp = pack_weight(n((K, N)) * 1 / np.sqrt(K) * fk[:, None], "e4m3")
    return {
        "xt_words": xtp[0],
        "xt_scales": xtp[1],
        "w_words": wp[0],
        "w_scales": wp[1],
        "w2_words": w2p[0],
        "w2_scales": w2p[1],
        "wb_words": wbp[0],
        "wb_scales": wbp[1],
        "ws_words": wsp[0],
        "ws_scales": wsp[1],
        "offs": striped(idx),
        "offs2": striped(idx2),
        "offs3": striped(idx3),
        "offs4": striped(idx4),
    }


def reference(xt_words, xt_scales, w_words, w_scales, w2_words, w2_scales, wb_words, wb_scales, ws_words, ws_scales, offs, offs2, offs3, offs4):
    idx = unstriped(offs)
    idx2 = unstriped(offs2)
    idx3 = unstriped(offs3)
    idx4 = unstriped(offs4)
    xtu = unpack_weight(xt_words, xt_scales, "e2m1")
    wu = unpack_weight(w_words, w_scales, "e5m2")
    w2u = unpack_weight(w2_words, w2_scales, "e4m3")
    wbu = unpack_weight(wb_words, wb_scales, "e4m3")
    wsu = unpack_weight(ws_words, ws_scales, "e4m3")
    xtidxg = xtu[:, idx]
    a = wu.T @ xtidxg
    xtidx2g = xtu[:, idx2]
    b = w2u.T @ xtidx2g
    pw = np.zeros((R, C))
    pw[:, idx3] = a
    hid = np.maximum(pw[:, idx4], b)
    hidq = mxq(hid, 0, "e5m2")
    y = wbu.T @ hidq + wsu.T @ xtidxg
    return y

@@ -1,0 +1,192 @@
+from contextlib import ExitStack
+
+import concourse.mybir as mybir
+
+K, T, J, R, C, N = 512, 2048, 256, 512, 512, 256
+FLOPS = 2 * K * J * (2 * R + N) + 2 * R * J * N
+
+F32 = mybir.dt.float32
+BF16 = mybir.dt.bfloat16
+I32 = mybir.dt.int32
+U32 = mybir.dt.uint32
+U16 = mybir.dt.uint16
+U8 = mybir.dt.uint8
+E2M1 = mybir.dt.float4_e2m1fn_x4
+E4M3 = mybir.dt.float8_e4m3fn_x4
+E5M2 = mybir.dt.float8_e5m2_x4
+COPY = mybir.ActivationFunctionType.Copy
+MAX = mybir.AluOpType.max
+
+P = 128
+PACK = 4
+QUADS = 4
+HALF = J // 2
+
+
+def tile_list_ahead_board_skip_plain_kernel(
+    tc, xt_words, xt_scales, w_words, w_scales, w2_words, w2_scales, wb_words, wb_scales,
+    ws_words, ws_scales, offs, offs2, offs3, offs4, out,
+):
+    nc = tc.nc
+    with ExitStack() as ctx:
+        sb = ctx.enter_context(tc.tile_pool(name="sb", bufs=1))
+        ps = ctx.enter_context(tc.psum_pool(name="ps", bufs=1))
+
+        def load_list(name, src):
+            lst = sb.tile([P, J // 16], U16, name=name)
+            nc.sync.dma_start(lst[:], src)
+            return lst
+
+        def zeroed_plane(name, width):
+            plane = sb.tile([P, width], U8, name=name, align_bytes=64)
+            nc.vector.memset(plane[:].bitcast(I32), 0)
+            return plane
+
+        def load_rows(plane, scales, q, queue):
+            queue.dma_start(
+                plane[32 * q : 32 * q + 4, :].bitcast(I32),
+                scales[0, 4 * q : 4 * q + 4, :].bitcast(I32),
+            )
+
+        def load_words(name, words, width, queue):
+            t = sb.tile([P, width], U32, name=name, align_bytes=64)
+            queue.dma_start(t[:].bitcast(I32), words[0].rearrange("p n t -> p (n t)").bitcast(I32))
+            return t
+
+        wsc = zeroed_plane("wsc", R)
+        xs = zeroed_plane("xs", T)
+        w2sc = zeroed_plane("w2sc", R)
+        wbsc = zeroed_plane("wbsc", N)
+        wssc = zeroed_plane("wssc", N)
+        board = [sb.tile([P, C], F32, name="board%d" % t) for t in range(PACK)]
+        for t in range(PACK):
+            nc.vector.memset(board[t][:], 0.0)
+
+        l1 = load_list("l1", offs)
+        for q in range(QUADS):
+            load_rows(wsc, w_scales, q, nc.sync if q < 2 else nc.scalar)
+        load_rows(xs, xt_scales, 0, nc.scalar)
+        xw = sb.tile([P, T], U16, name="xw", align_bytes=64)
+        nc.sync.dma_start(xw[:].bitcast(I32), xt_words[0].bitcast(I32))
+        ww = load_words("ww", w_words, R, nc.sync)
+        for q in range(1, QUADS):
+            load_rows(xs, xt_scales, q, nc.sync)
+        l2 = load_list("l2", offs2)
+        l3 = load_list("l3", offs3)
+        w2w = load_words("w2w", w2_words, R, nc.sync)
+        for q in range(QUADS):
+            load_rows(w2sc, w2_scales, q, nc.sync)
+        l4 = load_list("l4", offs4)
+        wsw = load_words("wsw", ws_words, N, nc.sync)
+        for q in range(QUADS):
+            load_rows(wssc, ws_scales, q, nc.sync)
+        wbw = load_words("wbw", wb_words, N, nc.sync)
+        for q in range(QUADS):
+            load_rows(wbsc, wb_scales, q, nc.sync)
+
+        def gather_tokens(name, lst):
+            gw = sb.tile([P, J], U16, name=name + "w", align_bytes=64)
+            nc.vector.tensor_copy(gw[:], xw[:].indirect(lst[:]))
+            gs = sb.tile([P, J], U8, name=name + "s", align_bytes=64)
+            nc.vector.tensor_copy(gs[:], xs[:].indirect(lst[:]))
+            return gw, gs
+
+        def deal_words(name, words):
+            dealt = sb.tile([P, R], U32, name=name, align_bytes=64)
+            nc.scalar.copy(
+                dealt[:].rearrange("p (t c i) -> p c t i", t=PACK, i=4),
+                words[:].rearrange("p (c i t) -> p c t i", t=PACK, i=4),
+            )
+            return dealt
+
+        def deal_scales(name, plane):
+            dealt = sb.tile([P, R], U8, name=name, align_bytes=64)
+            nc.vector.tensor_copy(
+                dealt[:].rearrange("p (t m) -> p t m", t=PACK),
+                plane[:].rearrange("p (m t) -> p t m", t=PACK),
+            )
+            return dealt
+
+        def first_stage(name, words, scales, fmt, gw, gs):
+            banks = [ps.tile([P, 2, J], F32, name="%s%d" % (name, u)) for u in range(2)]
+            for t in range(PACK):
+                cols = slice(t * P, (t + 1) * P)
+                nc.tensor.matmul_mx(
+                    banks[t // 2][:, t % 2, :],
+                    lhsT=words[:, cols].bitcast(fmt), lhsT_scale=scales[:, cols],
+                    rhs=gw[:].bitcast(E2M1), rhs_scale=gs[:], start=True, stop=True,
+                )
+            return banks
+
+        wsd = deal_scales("wsd", wsc)
+        x1w, x1s = gather_tokens("x1", l1)
+        wd = deal_words("wd", ww)
+        a_ps = first_stage("a", wd, wsd, E5M2, x1w, x1s)
+
+        a_sb = [sb.tile([P, 2, J], F32, name="a_sb%d" % u) for u in range(2)]
+        for u in range(2):
+            nc.scalar.activation(a_sb[u][:], a_ps[u][:], COPY)
+
+        x2w, x2s = gather_tokens("x2", l2)
+        w2sd = deal_scales("w2sd", w2sc)
+        w2d = deal_words("w2d", w2w)
+        b_ps = first_stage("b", w2d, w2sd, E4M3, x2w, x2s)
+
+        y_ps = [[ps.tile([P, HALF], F32, name="y%d%d" % (jh, h)) for h in range(2)] for jh in range(2)]
+        for jh in range(2):
+            js = slice(jh * HALF, (jh + 1) * HALF)
+            for h in range(2):
+                ns = slice(h * P, (h + 1) * P)
+                nc.tensor.matmul_mx(
+                    y_ps[jh][h][:],
+                    lhsT=wsw[:, ns].bitcast(E4M3), lhsT_scale=wssc[:, ns],
+                    rhs=x1w[:, js].bitcast(E2M1), rhs_scale=x1s[:, js], start=True, stop=False,
+                )
+
+        for t in range(2):
+            nc.vector.tensor_copy(board[t][:].indirect(l3[:]), a_sb[0][:, t, :])
+        for t in range(2):
+            nc.scalar.activation(board[2 + t][:].indirect(l3[:]), a_sb[1][:, t, :], COPY)
+
+        hid = [sb.tile([P, HALF, PACK], BF16, name="hid%d" % jh, align_bytes=64) for jh in range(2)]
+        got01 = sb.tile([P, 2, J], F32, name="got01")
+        for t in range(2):
+            nc.vector.tensor_copy(got01[:, t, :], board[t][:].indirect(l4[:]))
+        got23 = [sb.tile([P, 2, HALF], F32, name="got23%d" % jh) for jh in range(2)]
+        for jh in range(2):
+            cut = l4[:, jh * (HALF // 16) : (jh + 1) * (HALF // 16)]
+            for t in range(2):
+                nc.scalar.activation(got23[jh][:, t, :], board[2 + t][:].indirect(cut), COPY)
+
+        for jh in range(2):
+            js = slice(jh * HALF, (jh + 1) * HALF)
+            nc.vector.tensor_tensor(
+                hid[jh][:, :, 0:2], got01[:, :, js].rearrange("p t j -> p j t"),
+                b_ps[0][:, :, js].rearrange("p t j -> p j t"), MAX,
+            )
+        for jh in range(2):
+            js = slice(jh * HALF, (jh + 1) * HALF)
+            nc.vector.tensor_tensor(
+                hid[jh][:, :, 2:4], got23[jh][:].rearrange("p t j -> p j t"),
+                b_ps[1][:, :, js].rearrange("p t j -> p j t"), MAX,
+            )
+
+        out_v = out.rearrange("(h p) j -> p h j", p=P)
+        for jh in range(2):
+            js = slice(jh * HALF, (jh + 1) * HALF)
+            hw = sb.tile([P, HALF], U32, name="hw%d" % jh, align_bytes=64)
+            hs = sb.tile([P, HALF], U8, name="hs%d" % jh, align_bytes=64)
+            nc.vector.quantize_mx(hw[:].bitcast(E5M2), hs[:], hid[jh][:].rearrange("p j t -> p (j t)"))
+            y_sb = sb.tile([P, 2, HALF], F32, name="y_sb%d" % jh)
+            for h in range(2):
+                ns = slice(h * P, (h + 1) * P)
+                nc.tensor.matmul_mx(
+                    y_ps[jh][h][:],
+                    lhsT=wbw[:, ns].bitcast(E4M3), lhsT_scale=wbsc[:, ns],
+                    rhs=hw[:].bitcast(E5M2), rhs_scale=hs[:], start=False, stop=True,
+                )
+                if jh == 1 and h == 1:
+                    nc.vector.tensor_copy(y_sb[:, h, :], y_ps[jh][h][:])
+                else:
+                    nc.scalar.copy(y_sb[:, h, :], y_ps[jh][h][:])
+            nc.sync.dma_start(out_v[:, :, js], y_sb[:])

@@ -38,7 +38,7 @@ def tile_list_ahead_board_skip_plain_kernel(
             return lst
 
         def zeroed_plane(name, width):
-            plane = sb.tile([P, width], U8, name=name, align_bytes=64)
+            plane = sb.tile([P, width], U8, name=name, tag=name, align_bytes=64)
             nc.vector.memset(plane[:].bitcast(I32), 0)
             return plane
 
@@ -53,8 +53,10 @@ def tile_list_ahead_board_skip_plain_kernel(
             queue.dma_start(t[:].bitcast(I32), words[0].rearrange("p n t -> p (n t)").bitcast(I32))
             return t
 
+        xs = sb.tile([P, T], U8, name="xs", align_bytes=64)
+        nc.vector.memset(xs[:, : T // 2].bitcast(I32), 0)
+        nc.gpsimd.memset(xs[:, T // 2 :].bitcast(I32), 0)
         wsc = zeroed_plane("wsc", R)
-        xs = zeroed_plane("xs", T)
         w2sc = zeroed_plane("w2sc", R)
         wbsc = zeroed_plane("wbsc", N)
         wssc = zeroed_plane("wssc", N)
@@ -63,17 +65,16 @@ def tile_list_ahead_board_skip_plain_kernel(
             nc.vector.memset(board[t][:], 0.0)
 
         l1 = load_list("l1", offs)
+        l2 = load_list("l2", offs2)
         for q in range(QUADS):
-            load_rows(wsc, w_scales, q, nc.sync if q < 2 else nc.scalar)
-        load_rows(xs, xt_scales, 0, nc.scalar)
+            load_rows(xs, xt_scales, q, nc.scalar if q < 2 else nc.sync)
         xw = sb.tile([P, T], U16, name="xw", align_bytes=64)
         nc.sync.dma_start(xw[:].bitcast(I32), xt_words[0].bitcast(I32))
         ww = load_words("ww", w_words, R, nc.sync)
-        for q in range(1, QUADS):
-            load_rows(xs, xt_scales, q, nc.sync)
-        l2 = load_list("l2", offs2)
-        l3 = load_list("l3", offs3)
+        for q in range(QUADS):
+            load_rows(wsc, w_scales, q, nc.sync)
         w2w = load_words("w2w", w2_words, R, nc.sync)
+        l3 = load_list("l3", offs3)
         for q in range(QUADS):
             load_rows(w2sc, w2_scales, q, nc.sync)
         l4 = load_list("l4", offs4)
@@ -84,96 +85,94 @@ def tile_list_ahead_board_skip_plain_kernel(
         for q in range(QUADS):
             load_rows(wbsc, wb_scales, q, nc.sync)
 
-        def gather_tokens(name, lst):
-            gw = sb.tile([P, J], U16, name=name + "w", align_bytes=64)
-            nc.vector.tensor_copy(gw[:], xw[:].indirect(lst[:]))
-            gs = sb.tile([P, J], U8, name=name + "s", align_bytes=64)
-            nc.vector.tensor_copy(gs[:], xs[:].indirect(lst[:]))
-            return gw, gs
+        def gather(name, table, dtype, lst, tag=None):
+            picked = sb.tile([P, J], dtype, name=name, tag=tag or name, align_bytes=64)
+            nc.vector.tensor_copy(picked[:], table[:].indirect(lst[:]))
+            return picked
 
-        def deal_words(name, words):
-            dealt = sb.tile([P, R], U32, name=name, align_bytes=64)
-            nc.scalar.copy(
-                dealt[:].rearrange("p (t c i) -> p c t i", t=PACK, i=4),
-                words[:].rearrange("p (c i t) -> p c t i", t=PACK, i=4),
+        def deal_words(name, words, ts, copy, dtype):
+            n = ts.stop - ts.start
+            dealt = sb.tile([P, n * P], U32, name=name, align_bytes=64)
+            copy(
+                dealt[:].bitcast(dtype).rearrange("p (t c i) -> p c t i", t=n, i=4),
+                words[:].bitcast(dtype).rearrange("p (c i t) -> p c t i", t=PACK, i=4)[:, :, ts, :],
             )
-            return dealt
+            return [dealt[:, u * P : (u + 1) * P] for u in range(n)]
 
-        def deal_scales(name, plane):
-            dealt = sb.tile([P, R], U8, name=name, align_bytes=64)
+        def deal_scales(name, plane, ts):
+            n = ts.stop - ts.start
+            dealt = sb.tile([P, n * P], U8, name=name, align_bytes=64)
             nc.vector.tensor_copy(
-                dealt[:].rearrange("p (t m) -> p t m", t=PACK),
-                plane[:].rearrange("p (m t) -> p t m", t=PACK),
+                dealt[:].rearrange("p (t m) -> p t m", t=n),
+                plane[:].rearrange("p (m t) -> p t m", t=PACK)[:, ts, :],
             )
-            return dealt
+            return [dealt[:, u * P : (u + 1) * P] for u in range(n)]
 
-        def first_stage(name, words, scales, fmt, gw, gs):
-            banks = [ps.tile([P, 2, J], F32, name="%s%d" % (name, u)) for u in range(2)]
-            for t in range(PACK):
-                cols = slice(t * P, (t + 1) * P)
-                nc.tensor.matmul_mx(
-                    banks[t // 2][:, t % 2, :],
-                    lhsT=words[:, cols].bitcast(fmt), lhsT_scale=scales[:, cols],
-                    rhs=gw[:].bitcast(E2M1), rhs_scale=gs[:], start=True, stop=True,
-                )
-            return banks
+        def first_stage(acc, words, scales, fmt, gw, gs):
+            nc.tensor.matmul_mx(
+                acc, lhsT=words.bitcast(fmt), lhsT_scale=scales,
+                rhs=gw.bitcast(E2M1), rhs_scale=gs, start=True, stop=True,
+            )
 
-        wsd = deal_scales("wsd", wsc)
-        x1w, x1s = gather_tokens("x1", l1)
-        wd = deal_words("wd", ww)
-        a_ps = first_stage("a", wd, wsd, E5M2, x1w, x1s)
+        halves = [slice(jh * HALF, (jh + 1) * HALF) for jh in range(2)]
 
-        a_sb = [sb.tile([P, 2, J], F32, name="a_sb%d" % u) for u in range(2)]
+        x1s = gather("x1s", xs, U8, l1)
+        x2s = gather("x2s", xs, U8, l2)
+        x1w = gather("x1w", xw, U16, l1)
+        a_ps = [ps.tile([P, J], F32, name="a%d" % t, tag="bank%d" % t) for t in range(PACK)]
+        a_sb = [sb.tile([P, J], F32, name="a_sb%d" % t) for t in range(PACK)]
         for u in range(2):
-            nc.scalar.activation(a_sb[u][:], a_ps[u][:], COPY)
+            ts = slice(2 * u, 2 * u + 2)
+            wd = deal_words("wd%d" % u, ww, ts, nc.scalar.copy, U32)
+            wsd = deal_scales("wsd%d" % u, wsc, ts)
+            for e in range(2):
+                first_stage(a_ps[2 * u + e][:], wd[e], wsd[e], E5M2, x1w[:], x1s[:])
+        x2w = gather("x2w", xw, U16, l2, "wsc")
+        w2d = deal_words("w2d", w2w, slice(0, PACK), nc.vector.tensor_copy, I32)
 
-        x2w, x2s = gather_tokens("x2", l2)
-        w2sd = deal_scales("w2sd", w2sc)
-        w2d = deal_words("w2d", w2w)
-        b_ps = first_stage("b", w2d, w2sd, E4M3, x2w, x2s)
+        for t in range(3):
+            nc.scalar.activation(a_sb[t][:], a_ps[t][:], COPY)
+        nc.vector.tensor_copy(board[0][:].indirect(l3[:]), a_sb[0][:])
+        nc.scalar.activation(board[1][:].indirect(l3[:]), a_sb[1][:], COPY)
+        nc.scalar.activation(a_sb[3][:], a_ps[3][:], COPY)
+        w2sd = deal_scales("w2sd", w2sc, slice(0, PACK))
+        nc.vector.tensor_copy(board[2][:].indirect(l3[:]), a_sb[2][:])
+        nc.scalar.activation(board[3][:].indirect(l3[:]), a_sb[3][:], COPY)
 
-        y_ps = [[ps.tile([P, HALF], F32, name="y%d%d" % (jh, h)) for h in range(2)] for jh in range(2)]
+        b_ps = [ps.tile([P, PACK, HALF], F32, name="b%d" % jh) for jh in range(2)]
         for jh in range(2):
-            js = slice(jh * HALF, (jh + 1) * HALF)
+            for t in range(PACK):
+                first_stage(b_ps[jh][:, t, :], w2d[t], w2sd[t], E4M3, x2w[:, halves[jh]], x2s[:, halves[jh]])
+        y_ps = [
+            [ps.tile([P, HALF], F32, name="y%d%d" % (jh, h), tag="bank%d" % (2 * jh + h)) for h in range(2)]
+            for jh in range(2)
+        ]
+        for jh in range(2):
             for h in range(2):
                 ns = slice(h * P, (h + 1) * P)
                 nc.tensor.matmul_mx(
                     y_ps[jh][h][:],
                     lhsT=wsw[:, ns].bitcast(E4M3), lhsT_scale=wssc[:, ns],
-                    rhs=x1w[:, js].bitcast(E2M1), rhs_scale=x1s[:, js], start=True, stop=False,
+                    rhs=x1w[:, halves[jh]].bitcast(E2M1), rhs_scale=x1s[:, halves[jh]], start=True, stop=False,
                 )
 
-        for t in range(2):
-            nc.vector.tensor_copy(board[t][:].indirect(l3[:]), a_sb[0][:, t, :])
-        for t in range(2):
-            nc.scalar.activation(board[2 + t][:].indirect(l3[:]), a_sb[1][:, t, :], COPY)
-
-        hid = [sb.tile([P, HALF, PACK], BF16, name="hid%d" % jh, align_bytes=64) for jh in range(2)]
-        got01 = sb.tile([P, 2, J], F32, name="got01")
-        for t in range(2):
-            nc.vector.tensor_copy(got01[:, t, :], board[t][:].indirect(l4[:]))
-        got23 = [sb.tile([P, 2, HALF], F32, name="got23%d" % jh) for jh in range(2)]
+        got = [sb.tile([P, PACK, HALF], F32, name="got%d" % jh) for jh in range(2)]
         for jh in range(2):
             cut = l4[:, jh * (HALF // 16) : (jh + 1) * (HALF // 16)]
-            for t in range(2):
-                nc.scalar.activation(got23[jh][:, t, :], board[2 + t][:].indirect(cut), COPY)
+            for t in range(PACK):
+                if t % 2 == 0:
+                    nc.vector.tensor_copy(got[jh][:, t, :], board[t][:].indirect(cut))
+                else:
+                    nc.scalar.activation(got[jh][:, t, :], board[t][:].indirect(cut), COPY)
 
+        hid = [sb.tile([P, HALF, PACK], BF16, name="hid%d" % jh, align_bytes=64) for jh in range(2)]
         for jh in range(2):
-            js = slice(jh * HALF, (jh + 1) * HALF)
             nc.vector.tensor_tensor(
-                hid[jh][:, :, 0:2], got01[:, :, js].rearrange("p t j -> p j t"),
-                b_ps[0][:, :, js].rearrange("p t j -> p j t"), MAX,
-            )
-        for jh in range(2):
-            js = slice(jh * HALF, (jh + 1) * HALF)
-            nc.vector.tensor_tensor(
-                hid[jh][:, :, 2:4], got23[jh][:].rearrange("p t j -> p j t"),
-                b_ps[1][:, :, js].rearrange("p t j -> p j t"), MAX,
+                hid[jh][:], got[jh][:].rearrange("p t j -> p j t"), b_ps[jh][:].rearrange("p t j -> p j t"), MAX,
             )
 
         out_v = out.rearrange("(h p) j -> p h j", p=P)
         for jh in range(2):
-            js = slice(jh * HALF, (jh + 1) * HALF)
             hw = sb.tile([P, HALF], U32, name="hw%d" % jh, align_bytes=64)
             hs = sb.tile([P, HALF], U8, name="hs%d" % jh, align_bytes=64)
             nc.vector.quantize_mx(hw[:].bitcast(E5M2), hs[:], hid[jh][:].rearrange("p j t -> p (j t)"))
@@ -189,4 +188,4 @@ def tile_list_ahead_board_skip_plain_kernel(
                     nc.vector.tensor_copy(y_sb[:, h, :], y_ps[jh][h][:])
                 else:
                     nc.scalar.copy(y_sb[:, h, :], y_ps[jh][h][:])
-            nc.sync.dma_start(out_v[:, :, js], y_sb[:])
+            nc.sync.dma_start(out_v[:, :, halves[jh]], y_sb[:])

@@ -53,9 +53,7 @@ def tile_list_ahead_board_skip_plain_kernel(
             queue.dma_start(t[:].bitcast(I32), words[0].rearrange("p n t -> p (n t)").bitcast(I32))
             return t
 
-        xs = sb.tile([P, T], U8, name="xs", align_bytes=64)
-        nc.vector.memset(xs[:, : T // 2].bitcast(I32), 0)
-        nc.gpsimd.memset(xs[:, T // 2 :].bitcast(I32), 0)
+        xs = zeroed_plane("xs", T)
         wsc = zeroed_plane("wsc", R)
         w2sc = zeroed_plane("w2sc", R)
         wbsc = zeroed_plane("wbsc", N)
@@ -94,8 +92,8 @@ def tile_list_ahead_board_skip_plain_kernel(
             n = ts.stop - ts.start
             dealt = sb.tile([P, n * P], U32, name=name, align_bytes=64)
             copy(
-                dealt[:].bitcast(dtype).rearrange("p (t c i) -> p c t i", t=n, i=4),
-                words[:].bitcast(dtype).rearrange("p (c i t) -> p c t i", t=PACK, i=4)[:, :, ts, :],
+                dealt[:].bitcast(dtype).rearrange("p (t m) -> p m t", t=n),
+                words[:].bitcast(dtype).rearrange("p (m t) -> p m t", t=PACK)[:, :, ts],
             )
             return [dealt[:, u * P : (u + 1) * P] for u in range(n)]
 
@@ -168,7 +166,10 @@ def tile_list_ahead_board_skip_plain_kernel(
         hid = [sb.tile([P, HALF, PACK], BF16, name="hid%d" % jh, align_bytes=64) for jh in range(2)]
         for jh in range(2):
             nc.vector.tensor_tensor(
-                hid[jh][:], got[jh][:].rearrange("p t j -> p j t"), b_ps[jh][:].rearrange("p t j -> p j t"), MAX,
+                hid[jh][:].rearrange("p (c i) t -> p c t i", i=4),
+                got[jh][:].rearrange("p t (c i) -> p c t i", i=4),
+                b_ps[jh][:].rearrange("p t (c i) -> p c t i", i=4),
+                MAX,
             )
 
         out_v = out.rearrange("(h p) j -> p h j", p=P)

@@ -53,8 +53,8 @@ def tile_list_ahead_board_skip_plain_kernel(
             queue.dma_start(t[:].bitcast(I32), words[0].rearrange("p n t -> p (n t)").bitcast(I32))
             return t
 
-        xs = zeroed_plane("xs", T)
         wsc = zeroed_plane("wsc", R)
+        xs = zeroed_plane("xs", T)
         w2sc = zeroed_plane("w2sc", R)
         wbsc = zeroed_plane("wbsc", N)
         wssc = zeroed_plane("wssc", N)
@@ -63,14 +63,15 @@ def tile_list_ahead_board_skip_plain_kernel(
             nc.vector.memset(board[t][:], 0.0)
 
         l1 = load_list("l1", offs)
-        l2 = load_list("l2", offs2)
         for q in range(QUADS):
-            load_rows(xs, xt_scales, q, nc.scalar if q < 2 else nc.sync)
+            load_rows(wsc, w_scales, q, nc.scalar if q < 2 else nc.sync)
+        load_rows(xs, xt_scales, 0, nc.scalar)
         xw = sb.tile([P, T], U16, name="xw", align_bytes=64)
         nc.sync.dma_start(xw[:].bitcast(I32), xt_words[0].bitcast(I32))
         ww = load_words("ww", w_words, R, nc.sync)
-        for q in range(QUADS):
-            load_rows(wsc, w_scales, q, nc.sync)
+        for q in range(1, QUADS):
+            load_rows(xs, xt_scales, q, nc.sync)
+        l2 = load_list("l2", offs2)
         w2w = load_words("w2w", w2_words, R, nc.sync)
         l3 = load_list("l3", offs3)
         for q in range(QUADS):
@@ -83,8 +84,8 @@ def tile_list_ahead_board_skip_plain_kernel(
         for q in range(QUADS):
             load_rows(wbsc, wb_scales, q, nc.sync)
 
-        def gather(name, table, dtype, lst, tag=None):
-            picked = sb.tile([P, J], dtype, name=name, tag=tag or name, align_bytes=64)
+        def gather(name, table, dtype, lst):
+            picked = sb.tile([P, J], dtype, name=name, align_bytes=64)
             nc.vector.tensor_copy(picked[:], table[:].indirect(lst[:]))
             return picked
 
@@ -97,14 +98,10 @@ def tile_list_ahead_board_skip_plain_kernel(
             )
             return [dealt[:, u * P : (u + 1) * P] for u in range(n)]
 
-        def deal_scales(name, plane, ts):
-            n = ts.stop - ts.start
-            dealt = sb.tile([P, n * P], U8, name=name, align_bytes=64)
-            nc.vector.tensor_copy(
-                dealt[:].rearrange("p (t m) -> p t m", t=n),
-                plane[:].rearrange("p (m t) -> p t m", t=PACK)[:, ts, :],
-            )
-            return [dealt[:, u * P : (u + 1) * P] for u in range(n)]
+        def deal(name, src, dtype, copy):
+            dealt = sb.tile([P, R], dtype, name=name, align_bytes=64)
+            copy(dealt[:].rearrange("p (t m) -> p t m", t=PACK), src[:].rearrange("p (m t) -> p t m", t=PACK))
+            return [dealt[:, t * P : (t + 1) * P] for t in range(PACK)]
 
         def first_stage(acc, words, scales, fmt, gw, gs):
             nc.tensor.matmul_mx(
@@ -114,26 +111,24 @@ def tile_list_ahead_board_skip_plain_kernel(
 
         halves = [slice(jh * HALF, (jh + 1) * HALF) for jh in range(2)]
 
-        x1s = gather("x1s", xs, U8, l1)
-        x2s = gather("x2s", xs, U8, l2)
+        wsd = deal("wsd", wsc, U8, nc.vector.tensor_copy)
         x1w = gather("x1w", xw, U16, l1)
+        x1s = gather("x1s", xs, U8, l1)
         a_ps = [ps.tile([P, J], F32, name="a%d" % t, tag="bank%d" % t) for t in range(PACK)]
         a_sb = [sb.tile([P, J], F32, name="a_sb%d" % t) for t in range(PACK)]
         for u in range(2):
-            ts = slice(2 * u, 2 * u + 2)
-            wd = deal_words("wd%d" % u, ww, ts, nc.scalar.copy, U32)
-            wsd = deal_scales("wsd%d" % u, wsc, ts)
+            wd = deal_words("wd%d" % u, ww, slice(2 * u, 2 * u + 2), nc.scalar.copy, U32)
             for e in range(2):
-                first_stage(a_ps[2 * u + e][:], wd[e], wsd[e], E5M2, x1w[:], x1s[:])
-        x2w = gather("x2w", xw, U16, l2, "wsc")
-        w2d = deal_words("w2d", w2w, slice(0, PACK), nc.vector.tensor_copy, I32)
+                first_stage(a_ps[2 * u + e][:], wd[e], wsd[2 * u + e], E5M2, x1w[:], x1s[:])
+        x2w = gather("x2w", xw, U16, l2)
+        x2s = gather("x2s", xs, U8, l2)
+        w2d = deal("w2d", w2w, U32, nc.gpsimd.tensor_copy)
+        w2sd = deal("w2sd", w2sc, U8, nc.gpsimd.tensor_copy)
 
-        for t in range(3):
+        for t in range(PACK):
             nc.scalar.activation(a_sb[t][:], a_ps[t][:], COPY)
         nc.vector.tensor_copy(board[0][:].indirect(l3[:]), a_sb[0][:])
         nc.scalar.activation(board[1][:].indirect(l3[:]), a_sb[1][:], COPY)
-        nc.scalar.activation(a_sb[3][:], a_ps[3][:], COPY)
-        w2sd = deal_scales("w2sd", w2sc, slice(0, PACK))
         nc.vector.tensor_copy(board[2][:].indirect(l3[:]), a_sb[2][:])
         nc.scalar.activation(board[3][:].indirect(l3[:]), a_sb[3][:], COPY)
 

from contextlib import ExitStack

import concourse.mybir as mybir

K, T, J, R, C, N = 512, 2048, 256, 512, 512, 256
FLOPS = 2 * K * J * (2 * R + N) + 2 * R * J * N

F32 = mybir.dt.float32
BF16 = mybir.dt.bfloat16
I32 = mybir.dt.int32
U32 = mybir.dt.uint32
U16 = mybir.dt.uint16
U8 = mybir.dt.uint8
E2M1 = mybir.dt.float4_e2m1fn_x4
E4M3 = mybir.dt.float8_e4m3fn_x4
E5M2 = mybir.dt.float8_e5m2_x4
COPY = mybir.ActivationFunctionType.Copy
MAX = mybir.AluOpType.max

P = 128
PACK = 4
QUADS = 4
HALF = J // 2


def tile_list_ahead_board_skip_plain_kernel(
    tc, xt_words, xt_scales, w_words, w_scales, w2_words, w2_scales, wb_words, wb_scales,
    ws_words, ws_scales, offs, offs2, offs3, offs4, out,
):
    nc = tc.nc
    with ExitStack() as ctx:
        sb = ctx.enter_context(tc.tile_pool(name="sb", bufs=1))
        ps = ctx.enter_context(tc.psum_pool(name="ps", bufs=1))

        def load_list(name, src):
            lst = sb.tile([P, J // 16], U16, name=name)
            nc.sync.dma_start(lst[:], src)
            return lst

        def zeroed_plane(name, width):
            plane = sb.tile([P, width], U8, name=name, tag=name, align_bytes=64)
            nc.vector.memset(plane[:].bitcast(I32), 0)
            return plane

        def load_rows(plane, scales, q, queue):
            queue.dma_start(
                plane[32 * q : 32 * q + 4, :].bitcast(I32),
                scales[0, 4 * q : 4 * q + 4, :].bitcast(I32),
            )

        def load_words(name, words, width, queue):
            t = sb.tile([P, width], U32, name=name, align_bytes=64)
            queue.dma_start(t[:].bitcast(I32), words[0].rearrange("p n t -> p (n t)").bitcast(I32))
            return t

        wsc = zeroed_plane("wsc", R)
        xs = zeroed_plane("xs", T)
        w2sc = zeroed_plane("w2sc", R)
        wbsc = zeroed_plane("wbsc", N)
        wssc = zeroed_plane("wssc", N)
        board = [sb.tile([P, C], F32, name="board%d" % t) for t in range(PACK)]
        for t in range(PACK):
            nc.vector.memset(board[t][:], 0.0)

        l1 = load_list("l1", offs)
        for q in range(QUADS):
            load_rows(wsc, w_scales, q, nc.scalar if q < 2 else nc.sync)
        load_rows(xs, xt_scales, 0, nc.scalar)
        xw = sb.tile([P, T], U16, name="xw", align_bytes=64)
        nc.sync.dma_start(xw[:].bitcast(I32), xt_words[0].bitcast(I32))
        ww = load_words("ww", w_words, R, nc.sync)
        for q in range(1, QUADS):
            load_rows(xs, xt_scales, q, nc.sync)
        l2 = load_list("l2", offs2)
        w2w = load_words("w2w", w2_words, R, nc.sync)
        l3 = load_list("l3", offs3)
        for q in range(QUADS):
            load_rows(w2sc, w2_scales, q, nc.sync)
        l4 = load_list("l4", offs4)
        wsw = load_words("wsw", ws_words, N, nc.sync)
        for q in range(QUADS):
            load_rows(wssc, ws_scales, q, nc.sync)
        wbw = load_words("wbw", wb_words, N, nc.sync)
        for q in range(QUADS):
            load_rows(wbsc, wb_scales, q, nc.sync)

        def gather(name, table, dtype, lst):
            picked = sb.tile([P, J], dtype, name=name, align_bytes=64)
            nc.vector.tensor_copy(picked[:], table[:].indirect(lst[:]))
            return picked

        def deal_words(name, words, ts, copy, dtype):
            n = ts.stop - ts.start
            dealt = sb.tile([P, n * P], U32, name=name, align_bytes=64)
            copy(
                dealt[:].bitcast(dtype).rearrange("p (t m) -> p m t", t=n),
                words[:].bitcast(dtype).rearrange("p (m t) -> p m t", t=PACK)[:, :, ts],
            )
            return [dealt[:, u * P : (u + 1) * P] for u in range(n)]

        def deal(name, src, dtype, copy):
            dealt = sb.tile([P, R], dtype, name=name, align_bytes=64)
            copy(dealt[:].rearrange("p (t m) -> p t m", t=PACK), src[:].rearrange("p (m t) -> p t m", t=PACK))
            return [dealt[:, t * P : (t + 1) * P] for t in range(PACK)]

        def first_stage(acc, words, scales, fmt, gw, gs):
            nc.tensor.matmul_mx(
                acc, lhsT=words.bitcast(fmt), lhsT_scale=scales,
                rhs=gw.bitcast(E2M1), rhs_scale=gs, start=True, stop=True,
            )

        halves = [slice(jh * HALF, (jh + 1) * HALF) for jh in range(2)]

        wsd = deal("wsd", wsc, U8, nc.vector.tensor_copy)
        x1w = gather("x1w", xw, U16, l1)
        x1s = gather("x1s", xs, U8, l1)
        a_ps = [ps.tile([P, J], F32, name="a%d" % t, tag="bank%d" % t) for t in range(PACK)]
        a_sb = [sb.tile([P, J], F32, name="a_sb%d" % t) for t in range(PACK)]
        for u in range(2):
            wd = deal_words("wd%d" % u, ww, slice(2 * u, 2 * u + 2), nc.scalar.copy, U32)
            for e in range(2):
                first_stage(a_ps[2 * u + e][:], wd[e], wsd[2 * u + e], E5M2, x1w[:], x1s[:])
        x2w = gather("x2w", xw, U16, l2)
        x2s = gather("x2s", xs, U8, l2)
        w2d = deal("w2d", w2w, U32, nc.gpsimd.tensor_copy)
        w2sd = deal("w2sd", w2sc, U8, nc.gpsimd.tensor_copy)

        for t in range(PACK):
            nc.scalar.activation(a_sb[t][:], a_ps[t][:], COPY)
        nc.vector.tensor_copy(board[0][:].indirect(l3[:]), a_sb[0][:])
        nc.scalar.activation(board[1][:].indirect(l3[:]), a_sb[1][:], COPY)
        nc.vector.tensor_copy(board[2][:].indirect(l3[:]), a_sb[2][:])
        nc.scalar.activation(board[3][:].indirect(l3[:]), a_sb[3][:], COPY)

        b_ps = [ps.tile([P, PACK, HALF], F32, name="b%d" % jh) for jh in range(2)]
        for jh in range(2):
            for t in range(PACK):
                first_stage(b_ps[jh][:, t, :], w2d[t], w2sd[t], E4M3, x2w[:, halves[jh]], x2s[:, halves[jh]])
        y_ps = [
            [ps.tile([P, HALF], F32, name="y%d%d" % (jh, h), tag="bank%d" % (2 * jh + h)) for h in range(2)]
            for jh in range(2)
        ]
        for jh in range(2):
            for h in range(2):
                ns = slice(h * P, (h + 1) * P)
                nc.tensor.matmul_mx(
                    y_ps[jh][h][:],
                    lhsT=wsw[:, ns].bitcast(E4M3), lhsT_scale=wssc[:, ns],
                    rhs=x1w[:, halves[jh]].bitcast(E2M1), rhs_scale=x1s[:, halves[jh]], start=True, stop=False,
                )

        got = [sb.tile([P, PACK, HALF], F32, name="got%d" % jh) for jh in range(2)]
        for jh in range(2):
            cut = l4[:, jh * (HALF // 16) : (jh + 1) * (HALF // 16)]
            for t in range(PACK):
                if t % 2 == 0:
                    nc.vector.tensor_copy(got[jh][:, t, :], board[t][:].indirect(cut))
                else:
                    nc.scalar.activation(got[jh][:, t, :], board[t][:].indirect(cut), COPY)

        hid = [sb.tile([P, HALF, PACK], BF16, name="hid%d" % jh, align_bytes=64) for jh in range(2)]
        for jh in range(2):
            nc.vector.tensor_tensor(
                hid[jh][:].rearrange("p (c i) t -> p c t i", i=4),
                got[jh][:].rearrange("p t (c i) -> p c t i", i=4),
                b_ps[jh][:].rearrange("p t (c i) -> p c t i", i=4),
                MAX,
            )

        out_v = out.rearrange("(h p) j -> p h j", p=P)
        for jh in range(2):
            hw = sb.tile([P, HALF], U32, name="hw%d" % jh, align_bytes=64)
            hs = sb.tile([P, HALF], U8, name="hs%d" % jh, align_bytes=64)
            nc.vector.quantize_mx(hw[:].bitcast(E5M2), hs[:], hid[jh][:].rearrange("p j t -> p (j t)"))
            y_sb = sb.tile([P, 2, HALF], F32, name="y_sb%d" % jh)
            for h in range(2):
                ns = slice(h * P, (h + 1) * P)
                nc.tensor.matmul_mx(
                    y_ps[jh][h][:],
                    lhsT=wbw[:, ns].bitcast(E4M3), lhsT_scale=wbsc[:, ns],
                    rhs=hw[:].bitcast(E5M2), rhs_scale=hs[:], start=False, stop=True,
                )
                if jh == 1 and h == 1:
                    nc.vector.tensor_copy(y_sb[:, h, :], y_ps[jh][h][:])
                else:
                    nc.scalar.copy(y_sb[:, h, :], y_ps[jh][h][:])
            nc.sync.dma_start(out_v[:, :, halves[jh]], y_sb[:])
